import numpy as np
import ml_dtypes


def mxq(x, axis, fmt="e4m3"):
    dtype, down = {"e4m3": (ml_dtypes.float8_e4m3fn, 7), "e5m2": (ml_dtypes.float8_e5m2, 14)}[fmt]
    v = np.moveaxis(np.asarray(x, np.float32).astype(ml_dtypes.bfloat16).astype(np.float64), axis, -1)
    blocks = v.reshape(v.shape[:-1] + (-1, 32))
    amax = np.abs(blocks).max(-1, keepdims=True)
    byte = np.maximum(np.where(amax > 0, np.frexp(amax)[1] - 1 + 127, 0) - down, 1)
    scale = np.exp2(byte - 127.0)
    codes = (blocks / scale).astype(np.float32).astype(dtype).astype(np.float64)
    return np.moveaxis((codes * scale).reshape(v.shape), -1, axis)


WIDE = False


def mx_kscale(k):
    if not WIDE:
        return np.ones(k)
    levels = np.array([10, -10, 5, -5, 0])
    if k % 512:
        return np.exp2(np.random.permutation(np.resize(levels, k // 32))).repeat(32)
    a = np.empty((k // 512, 16))
    for p in range(k // 512):
        a[p, :8] = np.random.permutation(np.resize(levels, 8))
        for g in range(8):
            far = levels[np.abs(levels - a[p, g]) >= 10]
            a[p, g + 8] = far[np.random.randint(len(far))]
    return np.exp2(a.ravel()).repeat(32)


def f64(x):
    return np.asarray(x).astype(np.float64)


def striped(idx):
    return np.tile(idx.reshape(-1, 16).T, (8, 1)).astype(np.uint16)


def unstriped(offs):
    return offs[:16].T.reshape(-1).astype(np.int64)


def striped8(idx):
    return np.concatenate([x.reshape(-1, 16).T for x in idx]).astype(np.uint16)


def runs(offs, k):
    lists = np.stack([offs[16 * r : 16 * r + 16].T.reshape(-1) for r in range(8)]).astype(np.int64)
    return lists[np.arange(k) % 512 // 64]


def pack_weight(w):
    k, n = w.shape
    w = f64(np.asarray(w, np.float32).astype(ml_dtypes.bfloat16)).reshape(k // 32, 32, n)
    amax = np.abs(w).max(1)
    byte = np.clip(np.where(amax > 0, np.frexp(amax)[1] - 1 + 127 - 7, 1), 1, 254)
    scaled = (w * np.exp2(127.0 - byte)[:, None, :]).reshape(k, n).astype(np.float32)
    words = np.ascontiguousarray(scaled.reshape(k // 512, 128, 4, n).transpose(0, 1, 3, 2)).astype(ml_dtypes.float8_e4m3fn).view(np.uint8)
    return words, np.ascontiguousarray(byte.astype(np.uint8).reshape(k // 512, 16, n))


def unpack_weight(words, scales):
    g, p, n, _ = words.shape
    vals = np.ascontiguousarray(words).view(ml_dtypes.float8_e4m3fn).astype(np.float64) * np.repeat(np.exp2(scales.astype(np.float64) - 127.0), 8, axis=1)[..., None]
    return vals.transpose(0, 1, 3, 2).reshape(g * 512, n)


def sigmoid(v):
    return 1.0 / (1.0 + np.exp(-np.maximum(v, -700.0)))

def planes(y):
    n, m = y.shape
    v = y.astype(np.float32).astype(ml_dtypes.bfloat16).astype(np.float64).reshape(n // 32, 32, m)
    top = np.abs(v).max(1)
    byte = np.clip(np.where(top > 0, np.frexp(top)[1] - 1 + 127 - 7, 1), 1, 254)
    codes = (v * np.exp2(127.0 - byte)[:, None, :]).reshape(n, m).astype(np.float32).astype(ml_dtypes.float8_e4m3fn).view(np.uint8)
    words = codes.reshape(n // 512, 128, 4, m).transpose(0, 1, 3, 2)
    return np.ascontiguousarray(words), np.ascontiguousarray(byte.astype(np.uint8).reshape(n // 512, 16, m))


K, T, S, V, H = 512, 2048, 512, 512, 512


def setup_inputs():
    n = np.random.standard_normal
    s = mx_kscale(K)[:, None]
    u = mx_kscale(S)
    packed_xT = pack_weight(n((K, T)) * s)
    packed_w1 = pack_weight(n((K, H)) / np.sqrt(K) / s)
    packed_w2 = pack_weight(n((K, H)) / np.sqrt(K) / s)
    packed_w3 = pack_weight(n((K, H)) / np.sqrt(K) / s)
    return {
        "x_words": packed_xT[0],
        "x_scales": packed_xT[1],
        "w1_words": packed_w1[0],
        "w1_scales": packed_w1[1],
        "w2_words": packed_w2[0],
        "w2_scales": packed_w2[1],
        "w3_words": packed_w3[0],
        "w3_scales": packed_w3[1],
        "ga": (np.random.uniform(0.5, 1.5, (H, 1)) * u[:, None]).astype(np.float32),
        "gb": (np.random.uniform(0.5, 1.5, (H, 1)) / u[:, None]).astype(np.float32),
        "offs": striped(np.random.permutation(T)[:S]),
        "two": striped(np.random.permutation(T)[:S]),
        "n1": striped8(np.stack([np.random.permutation(S) for _ in range(8)])),
        "n2": striped8(np.stack([np.random.permutation(S) for _ in range(8)])),
        "three": striped(np.random.permutation(T)[:V]),
        "n3": striped8(np.stack([np.random.permutation(V) for _ in range(8)])),
        "n4": striped8(np.stack([np.random.permutation(V) for _ in range(8)])),
        "n5": striped8(np.stack([np.random.permutation(V) for _ in range(8)])),
        "n6": striped8(np.stack([np.random.permutation(V) for _ in range(8)])),
        "n7": striped8(np.stack([np.random.permutation(V) for _ in range(8)])),
    }


def reference(x_words, x_scales, w1_words, w1_scales, w2_words, w2_scales, w3_words, w3_scales, ga, gb, offs, two, n1, n2, three, n3, n4, n5, n6, n7):
    xq = unpack_weight(x_words, x_scales)[:, unstriped(offs)]
    y = unpack_weight(w1_words, w1_scales).T @ xq
    x_two = unpack_weight(x_words, x_scales)[:, unstriped(two)]
    d = unpack_weight(w2_words, w2_scales).T @ x_two
    z = f64(ga) * ((y + y[np.arange(H)[:, None], runs(n1, H)]) * (sigmoid(d + d[np.arange(H)[:, None], runs(n2, H)])))
    x_three = unpack_weight(x_words, x_scales)[:, unstriped(three)]
    b = unpack_weight(w3_words, w3_scales).T @ x_three
    sm = np.maximum(b, b[np.arange(H)[:, None], runs(n4, H)])
    ds = np.zeros((H, V))
    ds[np.arange(H)[:, None], runs(n3, H)] = sm
    z2 = f64(gb) * (ds * sigmoid(b))
    s = 0.0625 * ((mxq(z, 0, "e4m3").T @ mxq(z2, 0, "e4m3")))
    out_0 = (s[np.arange(S)[:, None], runs(n5, S)]) * sigmoid(s) + (s[np.arange(S)[:, None], runs(n6, S)]) * (sigmoid(s[np.arange(S)[:, None], runs(n7, S)]))
    return (out_0,) + planes(out_0)

@@ -1,0 +1,254 @@
+from contextlib import ExitStack
+
+import concourse.mybir as mybir
+
+F32 = mybir.dt.float32
+BF16 = mybir.dt.bfloat16
+I32 = mybir.dt.int32
+U32 = mybir.dt.uint32
+U16 = mybir.dt.uint16
+U8 = mybir.dt.uint8
+FP8X4 = mybir.dt.float8_e4m3fn_x4
+ALU = mybir.AluOpType
+ACT = mybir.ActivationFunctionType
+
+P = 128
+T = 2048
+N = 512
+R = 4
+FLOPS = 4 * 2 * 512 * 512 * 512
+PIECES = ((0, 256), (256, 512))
+
+
+def tile_picked_twktriebsendgwsum_none_po_kernel(
+    tc, x_words, x_scales, w1_words, w1_scales, w2_words, w2_scales, w3_words, w3_scales,
+    ga, gb, offs, two, n1, n2, three, n3, n4, n5, n6, n7, out_0, out_1, out_2,
+):
+    nc = tc.nc
+    with ExitStack() as ctx:
+        lists = ctx.enter_context(tc.tile_pool(name="lists", bufs=1))
+        keep = ctx.enter_context(tc.tile_pool(name="keep", bufs=1))
+        psum = ctx.enter_context(tc.psum_pool(name="psum", bufs=8))
+
+        def load_list(src, name):
+            tile = lists.tile([P, N // 16], U16, name=name)
+            nc.sync.dma_start(tile[:], src)
+            return tile
+
+        def new(name, shape, dtype, tag=None):
+            return keep.tile(shape, dtype, name=name, tag=tag or name, align_bytes=64)
+
+        def load_words(src, name):
+            tile = new(name, [P, src.shape[2]], I32)
+            nc.sync.dma_start(tile[:], src[0].rearrange("p n t -> p (n t)").bitcast(I32))
+            return tile
+
+        def load_scales(queue, tile, src, first):
+            for q in range(4):
+                queue.dma_start(
+                    tile[32 * q + first : 32 * q + first + 4, :].bitcast(I32),
+                    src[0, 4 * q : 4 * q + 4, :].bitcast(I32),
+                )
+
+        xs = new("xs", [P, T], U8)
+        w3s_raw = new("w3s_raw", [P, N], U8)
+        w12s_raw = new("w12s_raw", [P, N], U8)
+        nc.vector.memset(xs[:].bitcast(I32), 0)
+        nc.vector.memset(w3s_raw[:].bitcast(I32), 0)
+        nc.vector.memset(w12s_raw[:].bitcast(I32), 0)
+
+        three_t = load_list(three, "three_t")
+        offs_t = load_list(offs, "offs_t")
+        two_t = load_list(two, "two_t")
+        load_scales(nc.sync, xs, x_scales, 0)
+        xw = load_words(x_words, "xw")
+        w3_raw = load_words(w3_words, "w3_raw")
+        load_scales(nc.sync, w3s_raw, w3_scales, 0)
+        n4_t = load_list(n4, "n4_t")
+        n3_t = load_list(n3, "n3_t")
+        gb_t = new("gb_t", [P, R], F32)
+        nc.sync.dma_start(gb_t[:], gb.rearrange("(p t) o -> p (t o)", t=R))
+        w1_raw = load_words(w1_words, "w1_raw")
+        w2_raw = load_words(w2_words, "w2_raw")
+        load_scales(nc.sync, w12s_raw, w1_scales, 0)
+        load_scales(nc.sync, w12s_raw, w2_scales, 4)
+        ga_t = new("ga_t", [P, R], F32)
+        nc.sync.dma_start(ga_t[:], ga.rearrange("(p t) o -> p (t o)", t=R))
+        n2_t = load_list(n2, "n2_t")
+        n1_t = load_list(n1, "n1_t")
+        n5_t = load_list(n5, "n5_t")
+        n7_t = load_list(n7, "n7_t")
+        n6_t = load_list(n6, "n6_t")
+
+        def pick_scales(idx, name):
+            tile = new(name, [P, N], U8)
+            nc.vector.tensor_copy(tile[:], xs[:].indirect(idx[:]))
+            return tile
+
+        def pick_words(idx, name, tag=None):
+            tile = new(name, [P, N], U32, tag)
+            nc.vector.tensor_copy(tile[:], xw[:].bitcast(U32).indirect(idx[:]))
+            return tile
+
+        def deal(raw, name, dtype):
+            tile = new(name, [P, R, P], dtype)
+            nc.vector.tensor_copy(tile[:].rearrange("p t m -> p m t"), raw.rearrange("p (m t) -> p m t", t=R))
+            return tile
+
+        def product(name, lhs_w, lhs_s, rhs_w, rhs_s):
+            bank = psum.tile([P, N], F32, name=name, tag="bank")
+            nc.tensor.matmul_mx(
+                out=bank[:], lhsT=lhs_w.bitcast(FP8X4), lhsT_scale=lhs_s,
+                rhs=rhs_w.bitcast(FP8X4), rhs_scale=rhs_s, start=True, stop=True,
+            )
+            return bank
+
+        x3s = pick_scales(three_t, "x3s")
+        x1s = pick_scales(offs_t, "x1s")
+        x2s = pick_scales(two_t, "x2s")
+        x3w = pick_words(three_t, "x3w")
+        w3w = deal(w3_raw[:].bitcast(U32), "w3w", U32)
+        w3s = deal(w3s_raw[:], "w3s", U8)
+        x1w = pick_words(offs_t, "x1w", "w3_raw")
+        x2w = pick_words(two_t, "x2w", "w3s_raw")
+
+        b_win, b_dup = [], []
+        for t in range(R):
+            bank = product(f"b_bank{t}", w3w[:, t, :], w3s[:, t, :], x3w[:], x3s[:])
+            win = new(f"b_win{t}", [P, 2 * N], F32)
+            dup = new(f"b_dup{t}", [P, N], F32)
+            nc.scalar.activation(win[:, N:], bank[:], ACT.Sigmoid)
+            nc.scalar.copy(win[:, :N], bank[:])
+            nc.scalar.copy(dup[:], bank[:])
+            b_win.append(win)
+            b_dup.append(dup)
+
+        w1w = deal(w1_raw[:].bitcast(U32), "w1w", U32)
+        w2w = deal(w2_raw[:].bitcast(U32), "w2w", U32)
+        w12s = deal(w12s_raw[:], "w12s", U8)
+
+        z2_planes = new("z2_planes", [P, R, N], BF16)
+        excess, ds = [], []
+
+        def b_gather(t):
+            diff = new(f"b_diff{t}", [P, N], F32)
+            nc.vector.tensor_tensor(diff[:], b_win[t][:].indirect(n4_t[:]), b_dup[t][:], ALU.subtract)
+            ex = new(f"b_excess{t}", [P, N], F32)
+            nc.scalar.activation(ex[:], diff[:], ACT.Relu)
+            excess.append(ex)
+
+        def b_scatter(t):
+            win = new(f"ds{t}", [P, 2 * N], F32)
+            nc.vector.tensor_tensor(win[:].indirect(n3_t[:]), excess[t][:], b_dup[t][:], ALU.add)
+            ds.append(win)
+
+        def b_weigh(t):
+            nc.vector.scalar_tensor_tensor(
+                z2_planes[:, t, :], ds[t][:, :N], gb_t[:, t : t + 1], b_win[t][:, N:], ALU.mult, ALU.mult
+            )
+
+        y_win, d_win = [], []
+
+        def yd_products(t):
+            d_bank = product(f"d_bank{t}", w2w[:, t, :], w12s[4:, t, :], x2w[:], x2s[:])
+            y_bank = product(f"y_bank{t}", w1w[:, t, :], w12s[:, t, :], x1w[:], x1s[:])
+            yw = new(f"y_win{t}", [P, 2 * N], F32)
+            dw = new(f"d_win{t}", [P, 2 * N], F32)
+            nc.scalar.copy(dw[:, :N], d_bank[:])
+            nc.scalar.copy(yw[:, N:], d_bank[:])
+            nc.scalar.activation(yw[:, :N], y_bank[:], ACT.Copy, scale=ga_t[:, t : t + 1])
+            nc.scalar.activation(dw[:, N:], y_bank[:], ACT.Copy, scale=ga_t[:, t : t + 1])
+            y_win.append(yw)
+            d_win.append(dw)
+
+        b_gather(0)
+        for t in range(R):
+            if t + 1 < R:
+                b_gather(t + 1)
+            b_scatter(t)
+            if t > 0:
+                b_weigh(t - 1)
+            yd_products(t)
+
+        y_sum = new("y_sum", [P, R, N], F32)
+        gate = new("gate", [P, R, N], F32)
+
+        def d_gather(t):
+            d_sum = new(f"d_sum{t}", [P, N], F32)
+            nc.vector.tensor_tensor(d_sum[:], d_win[t][:].indirect(n2_t[:]), y_win[t][:, N:], ALU.add)
+            nc.scalar.activation(gate[:, t, :], d_sum[:], ACT.Sigmoid)
+
+        def y_gather(t):
+            nc.vector.tensor_tensor(y_sum[:, t, :], y_win[t][:].indirect(n1_t[:]), d_win[t][:, N:], ALU.add)
+
+        d_gather(0)
+        b_weigh(R - 1)
+        z2_woven = new("z2_woven", [P, N, R], BF16)
+        nc.scalar.copy(
+            z2_woven[:].rearrange("p (c i) t -> p c t i", i=4),
+            z2_planes[:].rearrange("p t (c i) -> p c t i", i=4),
+        )
+        for t in range(1, R):
+            d_gather(t)
+        for t in range(R - 1):
+            y_gather(t)
+        z2w = new("z2w", [P, N], U32)
+        z2s = new("z2s", [P, N], U8)
+        nc.vector.quantize_mx(out=z2w[:].bitcast(FP8X4), scales=z2s[:], in_=z2_woven[:].rearrange("p c t -> p (c t)"))
+        y_gather(R - 1)
+
+        s_banks = []
+        for pair in range(2):
+            woven = new(f"z_woven{pair}", [P, 2, P, R], BF16)
+            cols = slice(2 * pair, 2 * pair + 2)
+            nc.vector.tensor_tensor(
+                woven[:].rearrange("p u m t -> p m t u"),
+                y_sum[:].rearrange("p t (m u) -> p m t u", u=R)[:, :, :, cols],
+                gate[:].rearrange("p t (m u) -> p m t u", u=R)[:, :, :, cols],
+                ALU.mult,
+            )
+            zw = new(f"zw{pair}", [P, 2 * P], U32)
+            zs = new(f"zs{pair}", [P, 2 * P], U8)
+            nc.vector.quantize_mx(out=zw[:].bitcast(FP8X4), scales=zs[:], in_=woven[:].rearrange("p u m t -> p (u m t)"))
+            for u in range(2):
+                rows = slice(u * P, (u + 1) * P)
+                s_banks.append(product(f"s_bank{2 * pair + u}", zw[:, rows], zs[:, rows], z2w[:], z2s[:]))
+
+        out_rows = out_0.rearrange("(p t) v -> p t v", t=R)
+        out_words = out_1[0].rearrange("p n t -> p (n t)").bitcast(I32)
+        ow = new("ow", [P, N], U32)
+        osc = new("osc", [P, N], U8)
+        res = new("res", [P, R, N], F32)
+        halves = ((0, N // 2), (N // 2, N))
+
+        def planes(a, b, engine_copy):
+            woven = new(f"out_woven{a}", [P, b - a, R], BF16)
+            engine_copy(
+                woven[:].rearrange("p (c i) t -> p c t i", i=4),
+                res[:, :, a:b].rearrange("p t (c i) -> p c t i", i=4),
+            )
+            nc.vector.quantize_mx(
+                out=ow[:, a:b].bitcast(FP8X4), scales=osc[:, a:b], in_=woven[:].rearrange("p c t -> p (c t)")
+            )
+            nc.sync.dma_start(out_words[:, a:b], ow[:, a:b].bitcast(I32))
+
+        for t in range(R):
+            win = y_win[t]
+            sg = new(f"s_gate{t}", [P, N], F32)
+            nc.scalar.activation(win[:, :N], s_banks[t][:], ACT.Copy, scale=0.0625)
+            nc.scalar.activation(sg[:], s_banks[t][:], ACT.Sigmoid, scale=0.0625)
+            far = new(f"far{t}", [P, N], F32)
+            first = new(f"first{t}", [P, N], F32)
+            second = new(f"second{t}", [P, N], F32)
+            for a, b in halves if t == R - 1 else ((0, N),):
+                entries = slice(a // 16, b // 16)
+                nc.scalar.activation(far[:, a:b], win[:].indirect(n7_t[:, entries]), ACT.Sigmoid)
+                nc.vector.tensor_tensor(first[:, a:b], win[:].indirect(n5_t[:, entries]), sg[:, a:b], ALU.mult)
+                nc.vector.tensor_tensor(second[:, a:b], win[:].indirect(n6_t[:, entries]), far[:, a:b], ALU.mult)
+                nc.vector.tensor_tensor(res[:, t, a:b], first[:, a:b], second[:, a:b], ALU.add)
+                nc.sync.dma_start(out_rows[:, t, a:b], res[:, t, a:b])
+        planes(0, N // 2, nc.scalar.copy)
+        planes(N // 2, N, nc.vector.tensor_copy)
+        for q in range(4):
+            queue = nc.sync if q % 2 else nc.scalar
+            queue.dma_start(out_2[0, 4 * q : 4 * q + 4, :].bitcast(I32), osc[32 * q : 32 * q + 4, :].bitcast(I32))

@@ -57,12 +57,12 @@ def tile_picked_twktriebsendgwsum_none_po_kernel(
         nc.vector.memset(w3s_raw[:].bitcast(I32), 0)
         nc.vector.memset(w12s_raw[:].bitcast(I32), 0)
 
+        w3_raw = load_words(w3_words, "w3_raw")
         three_t = load_list(three, "three_t")
         offs_t = load_list(offs, "offs_t")
-        two_t = load_list(two, "two_t")
         load_scales(nc.sync, xs, x_scales, 0)
         xw = load_words(x_words, "xw")
-        w3_raw = load_words(w3_words, "w3_raw")
+        two_t = load_list(two, "two_t")
         load_scales(nc.sync, w3s_raw, w3_scales, 0)
         n4_t = load_list(n4, "n4_t")
         n3_t = load_list(n3, "n3_t")
@@ -103,25 +103,23 @@ def tile_picked_twktriebsendgwsum_none_po_kernel(
             )
             return bank
 
+        w3w = deal(w3_raw[:].bitcast(U32), "w3w", U32)
         x3s = pick_scales(three_t, "x3s")
         x1s = pick_scales(offs_t, "x1s")
         x2s = pick_scales(two_t, "x2s")
-        x3w = pick_words(three_t, "x3w")
-        w3w = deal(w3_raw[:].bitcast(U32), "w3w", U32)
         w3s = deal(w3s_raw[:], "w3s", U8)
-        x1w = pick_words(offs_t, "x1w", "w3_raw")
+        x3w = pick_words(three_t, "x3w")
+        x1w = pick_words(offs_t, "x1w")
         x2w = pick_words(two_t, "x2w", "w3s_raw")
 
-        b_win, b_dup = [], []
-        for t in range(R):
-            bank = product(f"b_bank{t}", w3w[:, t, :], w3s[:, t, :], x3w[:], x3s[:])
-            win = new(f"b_win{t}", [P, 2 * N], F32)
-            dup = new(f"b_dup{t}", [P, N], F32)
-            nc.scalar.activation(win[:, N:], bank[:], ACT.Sigmoid)
-            nc.scalar.copy(win[:, :N], bank[:])
-            nc.scalar.copy(dup[:], bank[:])
-            b_win.append(win)
-            b_dup.append(dup)
+        b_banks = [product(f"b_bank{t}", w3w[:, t, :], w3s[:, t, :], x3w[:], x3s[:]) for t in range(R)]
+        b_win = [new(f"b_win{t}", [P, 2 * N], F32) for t in range(R)]
+        b_dup = [b_win[t ^ 1][:, N:] for t in range(R)]
+        for t in range(0, R, 2):
+            nc.scalar.copy(b_win[t][:, :N], b_banks[t][:])
+            nc.scalar.copy(b_dup[t], b_banks[t][:])
+            nc.scalar.copy(b_dup[t + 1], b_banks[t + 1][:])
+            nc.scalar.copy(b_win[t + 1][:, :N], b_banks[t + 1][:])
 
         w1w = deal(w1_raw[:].bitcast(U32), "w1w", U32)
         w2w = deal(w2_raw[:].bitcast(U32), "w2w", U32)
@@ -132,19 +130,21 @@ def tile_picked_twktriebsendgwsum_none_po_kernel(
 
         def b_gather(t):
             diff = new(f"b_diff{t}", [P, N], F32)
-            nc.vector.tensor_tensor(diff[:], b_win[t][:].indirect(n4_t[:]), b_dup[t][:], ALU.subtract)
+            nc.vector.tensor_tensor(diff[:], b_win[t][:].indirect(n4_t[:]), b_dup[t], ALU.subtract)
             ex = new(f"b_excess{t}", [P, N], F32)
             nc.scalar.activation(ex[:], diff[:], ACT.Relu)
             excess.append(ex)
 
         def b_scatter(t):
             win = new(f"ds{t}", [P, 2 * N], F32)
-            nc.vector.tensor_tensor(win[:].indirect(n3_t[:]), excess[t][:], b_dup[t][:], ALU.add)
+            nc.vector.tensor_tensor(win[:].indirect(n3_t[:]), excess[t][:], b_dup[t], ALU.add)
             ds.append(win)
 
-        def b_weigh(t):
+        def b_weigh(t, tag):
+            b_gate = new(f"b_gate{t}", [P, N], F32, tag)
+            nc.scalar.activation(b_gate[:], b_banks[t][:], ACT.Sigmoid)
             nc.vector.scalar_tensor_tensor(
-                z2_planes[:, t, :], ds[t][:, :N], gb_t[:, t : t + 1], b_win[t][:, N:], ALU.mult, ALU.mult
+                z2_planes[:, t, :], ds[t][:, :N], gb_t[:, t : t + 1], b_gate[:], ALU.mult, ALU.mult
             )
 
         y_win, d_win = [], []
@@ -167,7 +167,7 @@ def tile_picked_twktriebsendgwsum_none_po_kernel(
                 b_gather(t + 1)
             b_scatter(t)
             if t > 0:
-                b_weigh(t - 1)
+                b_weigh(t - 1, f"b_diff{t}")
             yd_products(t)
 
         y_sum = new("y_sum", [P, R, N], F32)
@@ -182,22 +182,32 @@ def tile_picked_twktriebsendgwsum_none_po_kernel(
             nc.vector.tensor_tensor(y_sum[:, t, :], y_win[t][:].indirect(n1_t[:]), d_win[t][:, N:], ALU.add)
 
         d_gather(0)
-        b_weigh(R - 1)
+        d_gather(1)
+        b_weigh(R - 1, "d_sum0")
         z2_woven = new("z2_woven", [P, N, R], BF16)
         nc.scalar.copy(
             z2_woven[:].rearrange("p (c i) t -> p c t i", i=4),
             z2_planes[:].rearrange("p t (c i) -> p c t i", i=4),
         )
-        for t in range(1, R):
+        for t in range(2, R):
             d_gather(t)
-        for t in range(R - 1):
+        for t in range(R):
             y_gather(t)
-        z2w = new("z2w", [P, N], U32)
-        z2s = new("z2s", [P, N], U8)
-        nc.vector.quantize_mx(out=z2w[:].bitcast(FP8X4), scales=z2s[:], in_=z2_woven[:].rearrange("p c t -> p (c t)"))
-        y_gather(R - 1)
+        halves = ((0, N // 2), (N // 2, N))
+        z2w, z2s = [], []
+
+        def z2_quantize(h):
+            a, b = halves[h]
+            words = new(f"z2w{h}", [P, b - a], U32, f"d_win{R - 2 + h}")
+            scales = new(f"z2s{h}", [P, b - a], U8)
+            nc.vector.quantize_mx(
+                out=words[:].bitcast(FP8X4), scales=scales[:], in_=z2_woven[:, a:b, :].rearrange("p c t -> p (c t)")
+            )
+            z2w.append(words)
+            z2s.append(scales)
 
         s_banks = []
+        z2_quantize(0)
         for pair in range(2):
             woven = new(f"z_woven{pair}", [P, 2, P, R], BF16)
             cols = slice(2 * pair, 2 * pair + 2)
@@ -207,19 +217,31 @@ def tile_picked_twktriebsendgwsum_none_po_kernel(
                 gate[:].rearrange("p t (m u) -> p m t u", u=R)[:, :, :, cols],
                 ALU.mult,
             )
+            if pair == 0:
+                z2_quantize(1)
             zw = new(f"zw{pair}", [P, 2 * P], U32)
             zs = new(f"zs{pair}", [P, 2 * P], U8)
             nc.vector.quantize_mx(out=zw[:].bitcast(FP8X4), scales=zs[:], in_=woven[:].rearrange("p u m t -> p (u m t)"))
             for u in range(2):
                 rows = slice(u * P, (u + 1) * P)
-                s_banks.append(product(f"s_bank{2 * pair + u}", zw[:, rows], zs[:, rows], z2w[:], z2s[:]))
+                bank = psum.tile([P, N], F32, name=f"s_bank{2 * pair + u}", tag="bank")
+                for h, (a, b) in enumerate(halves):
+                    nc.tensor.matmul_mx(
+                        out=bank[:, a:b], lhsT=zw[:, rows].bitcast(FP8X4), lhsT_scale=zs[:, rows],
+                        rhs=z2w[h][:].bitcast(FP8X4), rhs_scale=z2s[h][:], start=True, stop=True,
+                    )
+                s_banks.append(bank)
 
         out_rows = out_0.rearrange("(p t) v -> p t v", t=R)
         out_words = out_1[0].rearrange("p n t -> p (n t)").bitcast(I32)
         ow = new("ow", [P, N], U32)
         osc = new("osc", [P, N], U8)
         res = new("res", [P, R, N], F32)
-        halves = ((0, N // 2), (N // 2, N))
+        s_gate = new("s_gate", [P, R, N], F32)
+        far = new("far", [P, R, N], F32)
+        first = new("first", [P, R, N], F32)
+        second = new("second", [P, R, N], F32)
+        last = R - 1
 
         def planes(a, b, engine_copy):
             woven = new(f"out_woven{a}", [P, b - a, R], BF16)
@@ -232,21 +254,32 @@ def tile_picked_twktriebsendgwsum_none_po_kernel(
             )
             nc.sync.dma_start(out_words[:, a:b], ow[:, a:b].bitcast(I32))
 
-        for t in range(R):
-            win = y_win[t]
-            sg = new(f"s_gate{t}", [P, N], F32)
-            nc.scalar.activation(win[:, :N], s_banks[t][:], ACT.Copy, scale=0.0625)
-            nc.scalar.activation(sg[:], s_banks[t][:], ACT.Sigmoid, scale=0.0625)
-            far = new(f"far{t}", [P, N], F32)
-            first = new(f"first{t}", [P, N], F32)
-            second = new(f"second{t}", [P, N], F32)
-            for a, b in halves if t == R - 1 else ((0, N),):
-                entries = slice(a // 16, b // 16)
-                nc.scalar.activation(far[:, a:b], win[:].indirect(n7_t[:, entries]), ACT.Sigmoid)
-                nc.vector.tensor_tensor(first[:, a:b], win[:].indirect(n5_t[:, entries]), sg[:, a:b], ALU.mult)
-                nc.vector.tensor_tensor(second[:, a:b], win[:].indirect(n6_t[:, entries]), far[:, a:b], ALU.mult)
-                nc.vector.tensor_tensor(res[:, t, a:b], first[:, a:b], second[:, a:b], ALU.add)
-                nc.sync.dma_start(out_rows[:, t, a:b], res[:, t, a:b])
+        def near_term(t, a, b):
+            if a == 0:
+                nc.scalar.activation(y_win[t][:, :N], s_banks[t][:], ACT.Copy, scale=0.0625)
+            nc.scalar.activation(s_gate[:, t, a:b], s_banks[t][:, a:b], ACT.Sigmoid, scale=0.0625)
+            looked_up = y_win[t][:].indirect(n5_t[:, a // 16 : b // 16])
+            nc.vector.tensor_tensor(first[:, t, a:b], looked_up, s_gate[:, t, a:b], ALU.mult)
+
+        def far_term(t, a, b):
+            nc.scalar.activation(far[:, t, a:b], y_win[t][:].indirect(n7_t[:, a // 16 : b // 16]), ACT.Sigmoid)
+            looked_up = y_win[t][:].indirect(n6_t[:, a // 16 : b // 16])
+            nc.vector.tensor_tensor(second[:, t, a:b], looked_up, far[:, t, a:b], ALU.mult)
+
+        def finish(tiles, a, b):
+            nc.vector.tensor_tensor(res[:, tiles, a:b], first[:, tiles, a:b], second[:, tiles, a:b], ALU.add)
+            nc.sync.dma_start(out_rows[:, tiles, a:b], res[:, tiles, a:b])
+
+        near_term(0, 0, N)
+        for t in range(last):
+            near_term(t + 1, 0, N if t + 1 < last else N // 2)
+            far_term(t, 0, N)
+        far_term(last, 0, N // 2)
+        finish(slice(0, last), 0, N)
+        finish(slice(last, R), 0, N // 2)
+        near_term(last, N // 2, N)
+        far_term(last, N // 2, N)
+        finish(slice(last, R), N // 2, N)
         planes(0, N // 2, nc.scalar.copy)
         planes(N // 2, N, nc.vector.tensor_copy)
         for q in range(4):

@@ -1,6 +1,7 @@
 from contextlib import ExitStack
 
 import concourse.mybir as mybir
+from concourse.masks import make_identity
 
 F32 = mybir.dt.float32
 BF16 = mybir.dt.bfloat16
@@ -56,6 +57,9 @@ def tile_picked_twktriebsendgwsum_none_po_kernel(
         nc.vector.memset(xs[:].bitcast(I32), 0)
         nc.vector.memset(w3s_raw[:].bitcast(I32), 0)
         nc.vector.memset(w12s_raw[:].bitcast(I32), 0)
+        identity = new("identity", [P, P], F32)
+        nc.vector.memset(identity[:], 0.0)
+        make_identity(nc, identity[:], nomemset=True)
 
         w3_raw = load_words(w3_words, "w3_raw")
         three_t = load_list(three, "three_t")
@@ -115,11 +119,14 @@ def tile_picked_twktriebsendgwsum_none_po_kernel(
         b_banks = [product(f"b_bank{t}", w3w[:, t, :], w3s[:, t, :], x3w[:], x3s[:]) for t in range(R)]
         b_win = [new(f"b_win{t}", [P, 2 * N], F32) for t in range(R)]
         b_dup = [b_win[t ^ 1][:, N:] for t in range(R)]
-        for t in range(0, R, 2):
+
+        def b_windows(t):
             nc.scalar.copy(b_win[t][:, :N], b_banks[t][:])
             nc.scalar.copy(b_dup[t], b_banks[t][:])
             nc.scalar.copy(b_dup[t + 1], b_banks[t + 1][:])
             nc.scalar.copy(b_win[t + 1][:, :N], b_banks[t + 1][:])
+
+        b_windows(0)
 
         w1w = deal(w1_raw[:].bitcast(U32), "w1w", U32)
         w2w = deal(w2_raw[:].bitcast(U32), "w2w", U32)
@@ -163,6 +170,8 @@ def tile_picked_twktriebsendgwsum_none_po_kernel(
 
         b_gather(0)
         for t in range(R):
+            if t == 1:
+                b_windows(2)
             if t + 1 < R:
                 b_gather(t + 1)
             b_scatter(t)
@@ -270,15 +279,37 @@ def tile_picked_twktriebsendgwsum_none_po_kernel(
             nc.vector.tensor_tensor(res[:, tiles, a:b], first[:, tiles, a:b], second[:, tiles, a:b], ALU.add)
             nc.sync.dma_start(out_rows[:, tiles, a:b], res[:, tiles, a:b])
 
+        def add_turned(t):
+            bank = psum.tile([P, N], F32, name=f"turned_bank{t}", tag="bank")
+            for c in range(0, N, P):
+                for term, opens in ((first, True), (second, False)):
+                    nc.tensor.matmul(
+                        bank[:, c : c + P], term[:, t, c : c + P], identity[:],
+                        is_transpose=True, start=opens, stop=not opens,
+                    )
+            turned = new(f"turned{t}", [P, N], F32)
+            nc.scalar.copy(turned[:], bank[:])
+            return turned
+
+        def turn_back(t, turned):
+            bank = psum.tile([P, N], F32, name=f"back_bank{t}", tag="bank")
+            for c in range(0, N, P):
+                nc.tensor.transpose(bank[:, c : c + P], turned[:, c : c + P], identity[:])
+            nc.scalar.copy(res[:, t, :], bank[:])
+            nc.sync.dma_start(out_rows[:, t, :], res[:, t, :])
+
         near_term(0, 0, N)
         for t in range(last):
             near_term(t + 1, 0, N if t + 1 < last else N // 2)
             far_term(t, 0, N)
         far_term(last, 0, N // 2)
-        finish(slice(0, last), 0, N)
+        finish(slice(2, last), 0, N)
         finish(slice(last, R), 0, N // 2)
         near_term(last, N // 2, N)
         far_term(last, N // 2, N)
+        turned = [add_turned(t) for t in range(2)]
+        for t in range(2):
+            turn_back(t, turned[t])
         finish(slice(last, R), N // 2, N)
         planes(0, N // 2, nc.scalar.copy)
         planes(N // 2, N, nc.vector.tensor_copy)

from contextlib import ExitStack

import concourse.mybir as mybir
from concourse.masks import make_identity

F32 = mybir.dt.float32
BF16 = mybir.dt.bfloat16
I32 = mybir.dt.int32
U32 = mybir.dt.uint32
U16 = mybir.dt.uint16
U8 = mybir.dt.uint8
FP8X4 = mybir.dt.float8_e4m3fn_x4
ALU = mybir.AluOpType
ACT = mybir.ActivationFunctionType

P = 128
T = 2048
N = 512
R = 4
FLOPS = 4 * 2 * 512 * 512 * 512
PIECES = ((0, 256), (256, 512))


def tile_picked_twktriebsendgwsum_none_po_kernel(
    tc, x_words, x_scales, w1_words, w1_scales, w2_words, w2_scales, w3_words, w3_scales,
    ga, gb, offs, two, n1, n2, three, n3, n4, n5, n6, n7, out_0, out_1, out_2,
):
    nc = tc.nc
    with ExitStack() as ctx:
        lists = ctx.enter_context(tc.tile_pool(name="lists", bufs=1))
        keep = ctx.enter_context(tc.tile_pool(name="keep", bufs=1))
        psum = ctx.enter_context(tc.psum_pool(name="psum", bufs=8))

        def load_list(src, name):
            tile = lists.tile([P, N // 16], U16, name=name)
            nc.sync.dma_start(tile[:], src)
            return tile

        def new(name, shape, dtype, tag=None):
            return keep.tile(shape, dtype, name=name, tag=tag or name, align_bytes=64)

        def load_words(src, name):
            tile = new(name, [P, src.shape[2]], I32)
            nc.sync.dma_start(tile[:], src[0].rearrange("p n t -> p (n t)").bitcast(I32))
            return tile

        def load_scales(queue, tile, src, first):
            for q in range(4):
                queue.dma_start(
                    tile[32 * q + first : 32 * q + first + 4, :].bitcast(I32),
                    src[0, 4 * q : 4 * q + 4, :].bitcast(I32),
                )

        xs = new("xs", [P, T], U8)
        w3s_raw = new("w3s_raw", [P, N], U8)
        w12s_raw = new("w12s_raw", [P, N], U8)
        nc.vector.memset(xs[:].bitcast(I32), 0)
        nc.vector.memset(w3s_raw[:].bitcast(I32), 0)
        nc.vector.memset(w12s_raw[:].bitcast(I32), 0)
        identity = new("identity", [P, P], F32)
        nc.vector.memset(identity[:], 0.0)
        make_identity(nc, identity[:], nomemset=True)

        w3_raw = load_words(w3_words, "w3_raw")
        three_t = load_list(three, "three_t")
        offs_t = load_list(offs, "offs_t")
        load_scales(nc.sync, xs, x_scales, 0)
        xw = load_words(x_words, "xw")
        two_t = load_list(two, "two_t")
        load_scales(nc.sync, w3s_raw, w3_scales, 0)
        n4_t = load_list(n4, "n4_t")
        n3_t = load_list(n3, "n3_t")
        gb_t = new("gb_t", [P, R], F32)
        nc.sync.dma_start(gb_t[:], gb.rearrange("(p t) o -> p (t o)", t=R))
        w1_raw = load_words(w1_words, "w1_raw")
        w2_raw = load_words(w2_words, "w2_raw")
        load_scales(nc.sync, w12s_raw, w1_scales, 0)
        load_scales(nc.sync, w12s_raw, w2_scales, 4)
        ga_t = new("ga_t", [P, R], F32)
        nc.sync.dma_start(ga_t[:], ga.rearrange("(p t) o -> p (t o)", t=R))
        n2_t = load_list(n2, "n2_t")
        n1_t = load_list(n1, "n1_t")
        n5_t = load_list(n5, "n5_t")
        n7_t = load_list(n7, "n7_t")
        n6_t = load_list(n6, "n6_t")

        def pick_scales(idx, name):
            tile = new(name, [P, N], U8)
            nc.vector.tensor_copy(tile[:], xs[:].indirect(idx[:]))
            return tile

        def pick_words(idx, name, tag=None):
            tile = new(name, [P, N], U32, tag)
            nc.vector.tensor_copy(tile[:], xw[:].bitcast(U32).indirect(idx[:]))
            return tile

        def deal(raw, name, dtype):
            tile = new(name, [P, R, P], dtype)
            nc.vector.tensor_copy(tile[:].rearrange("p t m -> p m t"), raw.rearrange("p (m t) -> p m t", t=R))
            return tile

        def product(name, lhs_w, lhs_s, rhs_w, rhs_s):
            bank = psum.tile([P, N], F32, name=name, tag="bank")
            nc.tensor.matmul_mx(
                out=bank[:], lhsT=lhs_w.bitcast(FP8X4), lhsT_scale=lhs_s,
                rhs=rhs_w.bitcast(FP8X4), rhs_scale=rhs_s, start=True, stop=True,
            )
            return bank

        w3w = deal(w3_raw[:].bitcast(U32), "w3w", U32)
        x3s = pick_scales(three_t, "x3s")
        x1s = pick_scales(offs_t, "x1s")
        x2s = pick_scales(two_t, "x2s")
        w3s = deal(w3s_raw[:], "w3s", U8)
        x3w = pick_words(three_t, "x3w")
        x1w = pick_words(offs_t, "x1w")
        x2w = pick_words(two_t, "x2w", "w3s_raw")

        b_banks = [product(f"b_bank{t}", w3w[:, t, :], w3s[:, t, :], x3w[:], x3s[:]) for t in range(R)]
        b_win = [new(f"b_win{t}", [P, 2 * N], F32) for t in range(R)]
        b_dup = [b_win[t ^ 1][:, N:] for t in range(R)]

        def b_windows(t):
            nc.scalar.copy(b_win[t][:, :N], b_banks[t][:])
            nc.scalar.copy(b_dup[t], b_banks[t][:])
            nc.scalar.copy(b_dup[t + 1], b_banks[t + 1][:])
            nc.scalar.copy(b_win[t + 1][:, :N], b_banks[t + 1][:])

        b_windows(0)

        w1w = deal(w1_raw[:].bitcast(U32), "w1w", U32)
        w2w = deal(w2_raw[:].bitcast(U32), "w2w", U32)
        w12s = deal(w12s_raw[:], "w12s", U8)

        z2_planes = new("z2_planes", [P, R, N], BF16)
        excess, ds = [], []

        def b_gather(t):
            diff = new(f"b_diff{t}", [P, N], F32)
            nc.vector.tensor_tensor(diff[:], b_win[t][:].indirect(n4_t[:]), b_dup[t], ALU.subtract)
            ex = new(f"b_excess{t}", [P, N], F32)
            nc.scalar.activation(ex[:], diff[:], ACT.Relu)
            excess.append(ex)

        def b_scatter(t):
            win = new(f"ds{t}", [P, 2 * N], F32)
            nc.vector.tensor_tensor(win[:].indirect(n3_t[:]), excess[t][:], b_dup[t], ALU.add)
            ds.append(win)

        def b_weigh(t, tag):
            b_gate = new(f"b_gate{t}", [P, N], F32, tag)
            nc.scalar.activation(b_gate[:], b_banks[t][:], ACT.Sigmoid)
            nc.vector.scalar_tensor_tensor(
                z2_planes[:, t, :], ds[t][:, :N], gb_t[:, t : t + 1], b_gate[:], ALU.mult, ALU.mult
            )

        y_win, d_win = [], []

        def yd_products(t):
            d_bank = product(f"d_bank{t}", w2w[:, t, :], w12s[4:, t, :], x2w[:], x2s[:])
            y_bank = product(f"y_bank{t}", w1w[:, t, :], w12s[:, t, :], x1w[:], x1s[:])
            yw = new(f"y_win{t}", [P, 2 * N], F32)
            dw = new(f"d_win{t}", [P, 2 * N], F32)
            nc.scalar.copy(dw[:, :N], d_bank[:])
            nc.scalar.copy(yw[:, N:], d_bank[:])
            nc.scalar.activation(yw[:, :N], y_bank[:], ACT.Copy, scale=ga_t[:, t : t + 1])
            nc.scalar.activation(dw[:, N:], y_bank[:], ACT.Copy, scale=ga_t[:, t : t + 1])
            y_win.append(yw)
            d_win.append(dw)

        b_gather(0)
        for t in range(R):
            if t == 1:
                b_windows(2)
            if t + 1 < R:
                b_gather(t + 1)
            b_scatter(t)
            if t > 0:
                b_weigh(t - 1, f"b_diff{t}")
            yd_products(t)

        y_sum = new("y_sum", [P, R, N], F32)
        gate = new("gate", [P, R, N], F32)

        def d_gather(t):
            d_sum = new(f"d_sum{t}", [P, N], F32)
            nc.vector.tensor_tensor(d_sum[:], d_win[t][:].indirect(n2_t[:]), y_win[t][:, N:], ALU.add)
            nc.scalar.activation(gate[:, t, :], d_sum[:], ACT.Sigmoid)

        def y_gather(t):
            nc.vector.tensor_tensor(y_sum[:, t, :], y_win[t][:].indirect(n1_t[:]), d_win[t][:, N:], ALU.add)

        d_gather(0)
        d_gather(1)
        b_weigh(R - 1, "d_sum0")
        z2_woven = new("z2_woven", [P, N, R], BF16)
        nc.scalar.copy(
            z2_woven[:].rearrange("p (c i) t -> p c t i", i=4),
            z2_planes[:].rearrange("p t (c i) -> p c t i", i=4),
        )
        for t in range(2, R):
            d_gather(t)
        for t in range(R):
            y_gather(t)
        halves = ((0, N // 2), (N // 2, N))
        z2w, z2s = [], []

        def z2_quantize(h):
            a, b = halves[h]
            words = new(f"z2w{h}", [P, b - a], U32, f"d_win{R - 2 + h}")
            scales = new(f"z2s{h}", [P, b - a], U8)
            nc.vector.quantize_mx(
                out=words[:].bitcast(FP8X4), scales=scales[:], in_=z2_woven[:, a:b, :].rearrange("p c t -> p (c t)")
            )
            z2w.append(words)
            z2s.append(scales)

        s_banks = []
        z2_quantize(0)
        for pair in range(2):
            woven = new(f"z_woven{pair}", [P, 2, P, R], BF16)
            cols = slice(2 * pair, 2 * pair + 2)
            nc.vector.tensor_tensor(
                woven[:].rearrange("p u m t -> p m t u"),
                y_sum[:].rearrange("p t (m u) -> p m t u", u=R)[:, :, :, cols],
                gate[:].rearrange("p t (m u) -> p m t u", u=R)[:, :, :, cols],
                ALU.mult,
            )
            if pair == 0:
                z2_quantize(1)
            zw = new(f"zw{pair}", [P, 2 * P], U32)
            zs = new(f"zs{pair}", [P, 2 * P], U8)
            nc.vector.quantize_mx(out=zw[:].bitcast(FP8X4), scales=zs[:], in_=woven[:].rearrange("p u m t -> p (u m t)"))
            for u in range(2):
                rows = slice(u * P, (u + 1) * P)
                bank = psum.tile([P, N], F32, name=f"s_bank{2 * pair + u}", tag="bank")
                for h, (a, b) in enumerate(halves):
                    nc.tensor.matmul_mx(
                        out=bank[:, a:b], lhsT=zw[:, rows].bitcast(FP8X4), lhsT_scale=zs[:, rows],
                        rhs=z2w[h][:].bitcast(FP8X4), rhs_scale=z2s[h][:], start=True, stop=True,
                    )
                s_banks.append(bank)

        out_rows = out_0.rearrange("(p t) v -> p t v", t=R)
        out_words = out_1[0].rearrange("p n t -> p (n t)").bitcast(I32)
        ow = new("ow", [P, N], U32)
        osc = new("osc", [P, N], U8)
        res = new("res", [P, R, N], F32)
        s_gate = new("s_gate", [P, R, N], F32)
        far = new("far", [P, R, N], F32)
        first = new("first", [P, R, N], F32)
        second = new("second", [P, R, N], F32)
        last = R - 1

        def planes(a, b, engine_copy):
            woven = new(f"out_woven{a}", [P, b - a, R], BF16)
            engine_copy(
                woven[:].rearrange("p (c i) t -> p c t i", i=4),
                res[:, :, a:b].rearrange("p t (c i) -> p c t i", i=4),
            )
            nc.vector.quantize_mx(
                out=ow[:, a:b].bitcast(FP8X4), scales=osc[:, a:b], in_=woven[:].rearrange("p c t -> p (c t)")
            )
            nc.sync.dma_start(out_words[:, a:b], ow[:, a:b].bitcast(I32))

        def near_term(t, a, b):
            if a == 0:
                nc.scalar.activation(y_win[t][:, :N], s_banks[t][:], ACT.Copy, scale=0.0625)
            nc.scalar.activation(s_gate[:, t, a:b], s_banks[t][:, a:b], ACT.Sigmoid, scale=0.0625)
            looked_up = y_win[t][:].indirect(n5_t[:, a // 16 : b // 16])
            nc.vector.tensor_tensor(first[:, t, a:b], looked_up, s_gate[:, t, a:b], ALU.mult)

        def far_term(t, a, b):
            nc.scalar.activation(far[:, t, a:b], y_win[t][:].indirect(n7_t[:, a // 16 : b // 16]), ACT.Sigmoid)
            looked_up = y_win[t][:].indirect(n6_t[:, a // 16 : b // 16])
            nc.vector.tensor_tensor(second[:, t, a:b], looked_up, far[:, t, a:b], ALU.mult)

        def finish(tiles, a, b):
            nc.vector.tensor_tensor(res[:, tiles, a:b], first[:, tiles, a:b], second[:, tiles, a:b], ALU.add)
            nc.sync.dma_start(out_rows[:, tiles, a:b], res[:, tiles, a:b])

        def add_turned(t):
            bank = psum.tile([P, N], F32, name=f"turned_bank{t}", tag="bank")
            for c in range(0, N, P):
                for term, opens in ((first, True), (second, False)):
                    nc.tensor.matmul(
                        bank[:, c : c + P], term[:, t, c : c + P], identity[:],
                        is_transpose=True, start=opens, stop=not opens,
                    )
            turned = new(f"turned{t}", [P, N], F32)
            nc.scalar.copy(turned[:], bank[:])
            return turned

        def turn_back(t, turned):
            bank = psum.tile([P, N], F32, name=f"back_bank{t}", tag="bank")
            for c in range(0, N, P):
                nc.tensor.transpose(bank[:, c : c + P], turned[:, c : c + P], identity[:])
            nc.scalar.copy(res[:, t, :], bank[:])
            nc.sync.dma_start(out_rows[:, t, :], res[:, t, :])

        near_term(0, 0, N)
        for t in range(last):
            near_term(t + 1, 0, N if t + 1 < last else N // 2)
            far_term(t, 0, N)
        far_term(last, 0, N // 2)
        finish(slice(2, last), 0, N)
        finish(slice(last, R), 0, N // 2)
        near_term(last, N // 2, N)
        far_term(last, N // 2, N)
        turned = [add_turned(t) for t in range(2)]
        for t in range(2):
            turn_back(t, turned[t])
        finish(slice(last, R), N // 2, N)
        planes(0, N // 2, nc.scalar.copy)
        planes(N // 2, N, nc.vector.tensor_copy)
        for q in range(4):
            queue = nc.sync if q % 2 else nc.scalar
            queue.dma_start(out_2[0, 4 * q : 4 * q + 4, :].bitcast(I32), osc[32 * q : 32 * q + 4, :].bitcast(I32))
